import numpy as np
import ml_dtypes


def mxq(x, axis, fmt="e4m3"):
    dtype, down = {"e4m3": (ml_dtypes.float8_e4m3fn, 7), "e5m2": (ml_dtypes.float8_e5m2, 14)}[fmt]
    v = np.moveaxis(np.asarray(x, np.float32).astype(ml_dtypes.bfloat16).astype(np.float64), axis, -1)
    blocks = v.reshape(v.shape[:-1] + (-1, 32))
    amax = np.abs(blocks).max(-1, keepdims=True)
    byte = np.maximum(np.where(amax > 0, np.frexp(amax)[1] - 1 + 127, 0) - down, 1)
    scale = np.exp2(byte - 127.0)
    codes = (blocks / scale).astype(np.float32).astype(dtype).astype(np.float64)
    return np.moveaxis((codes * scale).reshape(v.shape), -1, axis)


WIDE = False


def mx_kscale(k):
    if not WIDE:
        return np.ones(k)
    levels = np.array([10, -10, 5, -5, 0])
    if k % 512:
        return np.exp2(np.random.permutation(np.resize(levels, k // 32))).repeat(32)
    a = np.empty((k // 512, 16))
    for p in range(k // 512):
        a[p, :8] = np.random.permutation(np.resize(levels, 8))
        for g in range(8):
            far = levels[np.abs(levels - a[p, g]) >= 10]
            a[p, g + 8] = far[np.random.randint(len(far))]
    return np.exp2(a.ravel()).repeat(32)


def f64(x):
    return np.asarray(x).astype(np.float64)


def striped(idx):
    return np.tile(idx.reshape(-1, 16).T, (8, 1)).astype(np.uint16)


def unstriped(offs):
    return offs[:16].T.reshape(-1).astype(np.int64)


def striped8(idx):
    return np.concatenate([x.reshape(-1, 16).T for x in idx]).astype(np.uint16)


def runs(offs, k):
    lists = np.stack([offs[16 * r : 16 * r + 16].T.reshape(-1) for r in range(8)]).astype(np.int64)
    return lists[np.arange(k) % 512 // 64]


def pack_weight(w):
    k, n = w.shape
    w = f64(np.asarray(w, np.float32).astype(ml_dtypes.bfloat16)).reshape(k // 32, 32, n)
    amax = np.abs(w).max(1)
    byte = np.clip(np.where(amax > 0, np.frexp(amax)[1] - 1 + 127 - 7, 1), 1, 254)
    scaled = (w * np.exp2(127.0 - byte)[:, None, :]).reshape(k, n).astype(np.float32)
    words = np.ascontiguousarray(scaled.reshape(k // 512, 128, 4, n).transpose(0, 1, 3, 2)).astype(ml_dtypes.float8_e4m3fn).view(np.uint8)
    return words, np.ascontiguousarray(byte.astype(np.uint8).reshape(k // 512, 16, n))


def unpack_weight(words, scales):
    g, p, n, _ = words.shape
    vals = np.ascontiguousarray(words).view(ml_dtypes.float8_e4m3fn).astype(np.float64) * np.repeat(np.exp2(scales.astype(np.float64) - 127.0), 8, axis=1)[..., None]
    return vals.transpose(0, 1, 3, 2).reshape(g * 512, n)


K, T, S, V, N, H, U = 512, 2048, 1024, 512, 512, 512, 1024


def setup_inputs():
    n = np.random.standard_normal
    s = mx_kscale(K)[:, None]
    u = mx_kscale(H)
    packed_xT = pack_weight(n((K, T)) * s)
    return {
        "x_words": packed_xT[0],
        "x_scales": packed_xT[1],
        "w1": (n((K, H)) / np.sqrt(K) / s * u).astype(np.float32),
        "w2": (n((H, H)) / np.sqrt(H) / u[:, None] * u).astype(np.float32),
        "mem": (n((H, U)) * u[:, None]).astype(np.float32),
        "w3": (n((H, N)) / np.sqrt(H) / u[:, None]).astype(np.float32),
        "res": n((N, U)).astype(np.float32),
        "offs": striped(np.random.permutation(T)[:S]),
        "n1": striped8(np.stack([np.random.permutation(S) for _ in range(8)])),
        "n2": striped8(np.stack([np.random.permutation(U)[:V] for _ in range(8)])),
    }


def reference(x_words, x_scales, w1, w2, mem, w3, res, offs, n1, n2):
    xq = unpack_weight(x_words, x_scales)[:, unstriped(offs)]
    y = mxq(f64(w1), 0, "e4m3").T @ xq
    ln = y[np.arange(H)[:, None], runs(n1, H)]
    mx = ln.reshape(H, V, 2).max(axis=2)
    mn = ln.reshape(H, V, 2).min(axis=2)
    z = mx - (0.5 * mn)
    h = mxq(f64(w2), 0, "e4m3").T @ mxq(z, 0, "e4m3")
    z2 = f64(mem).copy()
    z2[np.arange(H)[:, None], runs(n2, H)] = h
    return f64(res) + (mxq(f64(w3), 0, "e4m3").T @ mxq(z2, 0, "e4m3"))

@@ -1,0 +1,217 @@
+from contextlib import ExitStack
+
+import concourse.mybir as mybir
+
+K, T, S, V, N, H, U = 512, 2048, 1024, 512, 512, 512, 1024
+FLOPS = 2 * K * H * S + 2 * H * H * V + 2 * H * N * U
+
+F32 = mybir.dt.float32
+BF16 = mybir.dt.bfloat16
+I32 = mybir.dt.int32
+U32 = mybir.dt.uint32
+U16 = mybir.dt.uint16
+U8 = mybir.dt.uint8
+FP8X4 = mybir.dt.float8_e4m3fn_x4
+ALU = mybir.AluOpType
+COPY = mybir.ActivationFunctionType.Copy
+
+P = 128
+PACK = 4
+BANK = 512
+OUT_CHUNKS = (128, 256, 256, 256, 128)
+
+
+def tile_picked_deeppgappage_none_p_kernel(
+    tc, x_words, x_scales, w1, w2, mem, w3, res, offs, n1, n2, out
+):
+    nc = tc.nc
+    with ExitStack() as ctx:
+        keep = ctx.enter_context(tc.tile_pool(name="keep", bufs=1))
+        psum = ctx.enter_context(tc.psum_pool(name="psum", bufs=1))
+
+        def sb(name, shape, dtype):
+            return keep.tile(shape, dtype, name=name, align_bytes=64)
+
+        def bank(i, shape):
+            return psum.tile(shape, F32, name="bank%d" % (i % 8))
+
+        def quantize(name, grouped, width):
+            codes = sb(name + "_codes", [P, width], U32)
+            scales = sb(name + "_scales", [P, width], U8)
+            nc.vector.quantize_mx(out=codes[:].bitcast(FP8X4), scales=scales[:], in_=grouped)
+            return codes, scales
+
+        def mm(dst, w, cols, rhs_codes, rhs_scales):
+            nc.tensor.matmul_mx(
+                out=dst,
+                lhsT=w[0][:, cols].bitcast(FP8X4),
+                lhsT_scale=w[1][:, cols],
+                rhs=rhs_codes.bitcast(FP8X4),
+                rhs_scale=rhs_scales,
+                start=True,
+                stop=True,
+            )
+
+        offs_t = keep.tile([P, S // 16], U16, name="offs_t")
+        n1_t = keep.tile([P, S // 16], U16, name="n1_t")
+        n2_t = keep.tile([P, V // 16], U16, name="n2_t")
+        xw = sb("xw", [P, T], U32)
+        xs = sb("xs", [P, T], U8)
+        nc.vector.memset(xs[:].bitcast(I32), 0)
+        nc.sync.dma_start(offs_t[:], offs)
+        for q in range(4):
+            nc.sync.dma_start(
+                out=xs[32 * q : 32 * q + 4, :].bitcast(I32),
+                in_=x_scales[0, 4 * q : 4 * q + 4, :].bitcast(I32),
+            )
+        nc.sync.dma_start(
+            out=xw[:].bitcast(I32), in_=x_words[0].rearrange("p n t -> p (n t)").bitcast(I32)
+        )
+        w1_raw = []
+        for h in range(2):
+            raw = sb("w1_raw%d" % h, [P, PACK, H // 2], F32)
+            nc.sync.dma_start(
+                out=raw[:], in_=w1.rearrange("(p j) c -> p j c", j=PACK)[:, :, h * 256 : (h + 1) * 256]
+            )
+            w1_raw.append(raw)
+        nc.sync.dma_start(n1_t[:], n1)
+        w2_raw = []
+        for h in range(2):
+            raw = sb("w2_raw%d" % h, [P, PACK, H // 2], F32)
+            nc.sync.dma_start(
+                out=raw[:], in_=w2.rearrange("(p j) c -> p j c", j=PACK)[:, :, h * 256 : (h + 1) * 256]
+            )
+            w2_raw.append(raw)
+        nc.sync.dma_start(n2_t[:], n2)
+        w3_raw = sb("w3_raw", [P, PACK, N], F32)
+        nc.sync.dma_start(out=w3_raw[:], in_=w3.rearrange("(p j) c -> p j c", j=PACK))
+        page = []
+        for t in range(PACK):
+            pg = sb("page%d" % t, [P, U], F32)
+            nc.sync.dma_start(out=pg[:], in_=mem.rearrange("(p t) w -> t p w", t=PACK)[t])
+            page.append(pg)
+        res_t = sb("res_t", [P, 4, U], F32)
+        nc.sync.dma_start(out=res_t[:], in_=res.rearrange("(t p) w -> p t w", p=P))
+
+        gs, gw = [], []
+        for h in range(2):
+            picks = offs_t[:, 32 * h : 32 * h + 32]
+            gs.append(sb("gs%d" % h, [P, BANK], U8))
+            nc.vector.tensor_copy(out=gs[h][:], in_=xs[:].indirect(picks))
+            gw.append(sb("gw%d" % h, [P, BANK], U32))
+            nc.vector.tensor_copy(out=gw[h][:], in_=xw[:].indirect(picks))
+
+        w1_bf = sb("w1_bf", [P, H * PACK], BF16)
+        w1_view = w1_bf[:].rearrange("p (t m j) -> p m j t", t=4, j=PACK)
+        for h in range(2):
+            nc.scalar.activation(
+                out=w1_view[:, 64 * h : 64 * h + 64],
+                in_=w1_raw[h][:].rearrange("p j (m t) -> p m j t", t=4),
+                func=COPY,
+            )
+        w1_q = quantize("w1", w1_bf[:], H)
+
+        y = [sb("y%d" % t, [P, S], F32) for t in range(PACK)]
+        for t, h in [(t, h) for t in range(PACK) for h in range(2)]:
+            b = bank(2 * t + h, [P, BANK])
+            mm(b[:], w1_q, slice(P * t, P * (t + 1)), gw[h][:], gs[h][:])
+            if h == 0:
+                nc.vector.tensor_copy(out=y[t][:, BANK * h : BANK * (h + 1)], in_=b[:])
+            else:
+                nc.scalar.copy(out=y[t][:, BANK * h : BANK * (h + 1)], in_=b[:])
+
+        ln = [sb("ln%d" % c, [P, PACK, 512], F32) for c in range(2)]
+        u = [sb("u%d" % c, [P, PACK, 256], F32) for c in range(2)]
+        w = [sb("w%d" % c, [P, PACK, 256], F32) for c in range(2)]
+        for c in range(2):
+            for t in range(PACK):
+                win = y[t][:].indirect(n1_t[:, 32 * c : 32 * c + 32])
+                if (c, t) in ((0, 0), (0, 1)):
+                    nc.vector.tensor_copy(out=ln[c][:, t, :], in_=win)
+                else:
+                    nc.scalar.activation(out=ln[c][:, t, :], in_=win, func=COPY)
+                if True:
+                    ts = slice(t, t + 1)
+                    pair = ln[c][:, ts, :].rearrange("p t (v e) -> p (t v) e", e=2)
+                    for dst, e in ((u[c], 0), (w[c], 1)):
+                        nc.vector.scalar_tensor_tensor(
+                            out=dst[:, ts, :].rearrange("p t v -> p (t v)"),
+                            in0=pair[:, :, 1 - e],
+                            scalar=-0.5,
+                            in1=pair[:, :, e],
+                            op0=ALU.mult,
+                            op1=ALU.add,
+                        )
+
+        w2_bf = sb("w2_bf", [P, H * PACK], BF16)
+        w2_view = w2_bf[:].rearrange("p (t m j) -> p m j t", t=4, j=PACK)
+        for h in range(2):
+            nc.scalar.copy(
+                out=w2_view[:, 64 * h : 64 * h + 64],
+                in_=w2_raw[h][:].rearrange("p j (m t) -> p m j t", t=4),
+            )
+        w2_q = quantize("w2", w2_bf[:], H)
+
+        hb = [bank(t, [P, 2, 256]) for t in range(PACK)]
+        hs = [sb("h%d" % t, [P, V], F32) for t in range(PACK)]
+        for c in range(2):
+            z_bf = sb("z_bf%d" % c, [P, 256 * PACK], BF16)
+            nc.vector.tensor_tensor(
+                out=z_bf[:].rearrange("p (c i t) -> p c t i", i=4, t=PACK),
+                in0=u[c][:].rearrange("p t (c i) -> p c t i", i=4),
+                in1=w[c][:].rearrange("p t (c i) -> p c t i", i=4),
+                op=ALU.max,
+            )
+            z_q = quantize("z%d" % c, z_bf[:], 256)
+            for t in range(PACK):
+                mm(hb[t][:, c, :], w2_q, slice(P * t, P * (t + 1)), z_q[0][:], z_q[1][:])
+            nc.scalar.copy(out=hs[0][:, 256 * c : 256 * (c + 1)], in_=hb[0][:, c, :])
+        for t in range(1, PACK):
+            nc.scalar.copy(out=hs[t][:], in_=hb[t][:].rearrange("p c v -> p (c v)"))
+
+        w3_bf = sb("y3", [P, N * PACK], BF16)
+        nc.scalar.copy(
+            out=w3_bf[:].rearrange("p (c i j) -> p c j i", i=4, j=PACK),
+            in_=w3_raw[:].rearrange("p j (c i) -> p c j i", i=4),
+        )
+        w3_q = quantize("w3", w3_bf[:], N)
+
+        starts = [sum(OUT_CHUNKS[:k]) for k in range(len(OUT_CHUNKS))]
+        z2_bf = sb("z2_bf", [P, U, PACK], BF16)
+        for t in range(PACK):
+            if t == 0:
+                for c in range(2):
+                    nc.vector.tensor_copy(
+                        out=page[t][:].indirect(n2_t[:, 16 * c : 16 * c + 16]),
+                        in_=hs[t][:, 256 * c : 256 * (c + 1)],
+                    )
+            else:
+                nc.vector.tensor_copy(out=page[t][:].indirect(n2_t[:]), in_=hs[t][:])
+            if t < PACK - 1:
+                nc.scalar.copy(out=z2_bf[:, :, t], in_=page[t][:])
+            else:
+                for k, wd in enumerate(OUT_CHUNKS):
+                    cols = slice(starts[k], starts[k] + wd)
+                    nc.scalar.copy(out=z2_bf[:, cols, t], in_=page[t][:, cols])
+
+        out_view = out.rearrange("(t p) w -> p t w", p=P)
+        sums = []
+        nb = 4
+        for k, wd in enumerate(OUT_CHUNKS):
+            cols = slice(starts[k], starts[k] + wd)
+            z2_q = quantize("z2_%d" % k, z2_bf[:, cols, :].rearrange("p w t -> p (w t)"), wd)
+            per = BANK // wd
+            for m0 in range(0, 4, per):
+                b = bank(nb, [P, per, wd])
+                nb = nb + 1
+                for i in range(per):
+                    mm(b[:, i, :], w3_q, slice(P * (m0 + i), P * (m0 + i + 1)), z2_q[0][:], z2_q[1][:])
+                sums.append((k, m0, per, b))
+        o = [sb("o%d" % k, [P, 4, wd], F32) for k, wd in enumerate(OUT_CHUNKS)]
+        for k, m0, per, b in sums:
+            cols = slice(starts[k], starts[k] + OUT_CHUNKS[k])
+            nc.vector.tensor_tensor(
+                out=o[k][:, m0 : m0 + per, :], in0=b[:], in1=res_t[:, m0 : m0 + per, cols], op=ALU.add
+            )
+            if m0 + per == 4:
+                nc.sync.dma_start(out=out_view[:, :, cols], in_=o[k][:])

@@ -35,8 +35,8 @@ def tile_picked_deeppgappage_none_p_kernel(
         def bank(i, shape):
             return psum.tile(shape, F32, name="bank%d" % (i % 8))
 
-        def quantize(name, grouped, width):
-            codes = sb(name + "_codes", [P, width], U32)
+        def quantize(name, grouped, width, codes_name=None):
+            codes = sb(codes_name or name + "_codes", [P, width], U32)
             scales = sb(name + "_scales", [P, width], U8)
             nc.vector.quantize_mx(out=codes[:].bitcast(FP8X4), scales=scales[:], in_=grouped)
             return codes, scales
@@ -94,12 +94,12 @@ def tile_picked_deeppgappage_none_p_kernel(
         nc.sync.dma_start(out=res_t[:], in_=res.rearrange("(t p) w -> p t w", p=P))
 
         gs, gw = [], []
+        picks = [offs_t[:, 32 * h : 32 * h + 32] for h in range(2)]
         for h in range(2):
-            picks = offs_t[:, 32 * h : 32 * h + 32]
-            gs.append(sb("gs%d" % h, [P, BANK], U8))
-            nc.vector.tensor_copy(out=gs[h][:], in_=xs[:].indirect(picks))
             gw.append(sb("gw%d" % h, [P, BANK], U32))
-            nc.vector.tensor_copy(out=gw[h][:], in_=xw[:].indirect(picks))
+            nc.vector.tensor_copy(out=gw[h][:], in_=xw[:].indirect(picks[h]))
+        gs.append(sb("gs0", [P, BANK], U8))
+        nc.vector.tensor_copy(out=gs[0][:], in_=xs[:].indirect(picks[0]))
 
         w1_bf = sb("w1_bf", [P, H * PACK], BF16)
         w1_view = w1_bf[:].rearrange("p (t m j) -> p m j t", t=4, j=PACK)
@@ -110,15 +110,29 @@ def tile_picked_deeppgappage_none_p_kernel(
                 func=COPY,
             )
         w1_q = quantize("w1", w1_bf[:], H)
+        gs.append(sb("w1_bf", [P, BANK], U8))
+        nc.vector.tensor_copy(out=gs[1][:], in_=xs[:].indirect(picks[1]))
 
         y = [sb("y%d" % t, [P, S], F32) for t in range(PACK)]
-        for t, h in [(t, h) for t in range(PACK) for h in range(2)]:
+        for t, h in [(0, 0), (1, 0), (0, 1), (1, 1), (2, 0), (2, 1), (3, 0), (3, 1)]:
             b = bank(2 * t + h, [P, BANK])
             mm(b[:], w1_q, slice(P * t, P * (t + 1)), gw[h][:], gs[h][:])
-            if h == 0:
+            if h == 0 and t > 1:
                 nc.vector.tensor_copy(out=y[t][:, BANK * h : BANK * (h + 1)], in_=b[:])
             else:
                 nc.scalar.copy(out=y[t][:, BANK * h : BANK * (h + 1)], in_=b[:])
+
+        w2_bf = sb("w2_bf", [P, H * PACK], BF16)
+        w2_view = w2_bf[:].rearrange("p (t m j) -> p m j t", t=4, j=PACK)
+        for h in range(2):
+            nc.scalar.copy(
+                out=w2_view[:, 64 * h : 64 * h + 64],
+                in_=w2_raw[h][:].rearrange("p j (m t) -> p m j t", t=4),
+            )
+        w2_q = quantize("w2", w2_bf[:], H)
+
+        hb = [bank(t, [P, 2, 256]) for t in range(PACK)]
+        hs = [sb("h%d" % t, [P, V], F32) for t in range(PACK)]
 
         ln = [sb("ln%d" % c, [P, PACK, 512], F32) for c in range(2)]
         u = [sb("u%d" % c, [P, PACK, 256], F32) for c in range(2)]
@@ -126,7 +140,7 @@ def tile_picked_deeppgappage_none_p_kernel(
         for c in range(2):
             for t in range(PACK):
                 win = y[t][:].indirect(n1_t[:, 32 * c : 32 * c + 32])
-                if (c, t) in ((0, 0), (0, 1)):
+                if c == 0 and t < 2:
                     nc.vector.tensor_copy(out=ln[c][:, t, :], in_=win)
                 else:
                     nc.scalar.activation(out=ln[c][:, t, :], in_=win, func=COPY)
@@ -142,24 +156,11 @@ def tile_picked_deeppgappage_none_p_kernel(
                             op0=ALU.mult,
                             op1=ALU.add,
                         )
-
-        w2_bf = sb("w2_bf", [P, H * PACK], BF16)
-        w2_view = w2_bf[:].rearrange("p (t m j) -> p m j t", t=4, j=PACK)
-        for h in range(2):
-            nc.scalar.copy(
-                out=w2_view[:, 64 * h : 64 * h + 64],
-                in_=w2_raw[h][:].rearrange("p j (m t) -> p m j t", t=4),
-            )
-        w2_q = quantize("w2", w2_bf[:], H)
-
-        hb = [bank(t, [P, 2, 256]) for t in range(PACK)]
-        hs = [sb("h%d" % t, [P, V], F32) for t in range(PACK)]
-        for c in range(2):
             z_bf = sb("z_bf%d" % c, [P, 256 * PACK], BF16)
             nc.vector.tensor_tensor(
-                out=z_bf[:].rearrange("p (c i t) -> p c t i", i=4, t=PACK),
-                in0=u[c][:].rearrange("p t (c i) -> p c t i", i=4),
-                in1=w[c][:].rearrange("p t (c i) -> p c t i", i=4),
+                out=z_bf[:].rearrange("p (c i t) -> p c t i", i=2, t=PACK),
+                in0=u[c][:].rearrange("p t (c i) -> p c t i", i=2),
+                in1=w[c][:].rearrange("p t (c i) -> p c t i", i=2),
                 op=ALU.max,
             )
             z_q = quantize("z%d" % c, z_bf[:], 256)
@@ -171,22 +172,14 @@ def tile_picked_deeppgappage_none_p_kernel(
 
         w3_bf = sb("y3", [P, N * PACK], BF16)
         nc.scalar.copy(
-            out=w3_bf[:].rearrange("p (c i j) -> p c j i", i=4, j=PACK),
-            in_=w3_raw[:].rearrange("p j (c i) -> p c j i", i=4),
+            out=w3_bf[:].rearrange("p (c i j) -> p c j i", i=2, j=PACK),
+            in_=w3_raw[:].rearrange("p j (c i) -> p c j i", i=2),
         )
-        w3_q = quantize("w3", w3_bf[:], N)
 
         starts = [sum(OUT_CHUNKS[:k]) for k in range(len(OUT_CHUNKS))]
         z2_bf = sb("z2_bf", [P, U, PACK], BF16)
         for t in range(PACK):
-            if t == 0:
-                for c in range(2):
-                    nc.vector.tensor_copy(
-                        out=page[t][:].indirect(n2_t[:, 16 * c : 16 * c + 16]),
-                        in_=hs[t][:, 256 * c : 256 * (c + 1)],
-                    )
-            else:
-                nc.vector.tensor_copy(out=page[t][:].indirect(n2_t[:]), in_=hs[t][:])
+            nc.vector.tensor_copy(out=page[t][:].indirect(n2_t[:]), in_=hs[t][:])
             if t < PACK - 1:
                 nc.scalar.copy(out=z2_bf[:, :, t], in_=page[t][:])
             else:
@@ -194,6 +187,7 @@ def tile_picked_deeppgappage_none_p_kernel(
                     cols = slice(starts[k], starts[k] + wd)
                     nc.scalar.copy(out=z2_bf[:, cols, t], in_=page[t][:, cols])
 
+        w3_q = quantize("w3", w3_bf[:], N, "h3")
         out_view = out.rearrange("(t p) w -> p t w", p=P)
         sums = []
         nb = 4
@@ -213,5 +207,4 @@ def tile_picked_deeppgappage_none_p_kernel(
             nc.vector.tensor_tensor(
                 out=o[k][:, m0 : m0 + per, :], in0=b[:], in1=res_t[:, m0 : m0 + per, cols], op=ALU.add
             )
-            if m0 + per == 4:
-                nc.sync.dma_start(out=out_view[:, :, cols], in_=o[k][:])
+            nc.sync.dma_start(out=out_view[:, m0 : m0 + per, cols], in_=o[k][:, m0 : m0 + per, :])

@@ -95,11 +95,11 @@ def tile_picked_deeppgappage_none_p_kernel(
 
         gs, gw = [], []
         picks = [offs_t[:, 32 * h : 32 * h + 32] for h in range(2)]
-        for h in range(2):
-            gw.append(sb("gw%d" % h, [P, BANK], U32))
-            nc.vector.tensor_copy(out=gw[h][:], in_=xw[:].indirect(picks[h]))
-        gs.append(sb("gs0", [P, BANK], U8))
-        nc.vector.tensor_copy(out=gs[0][:], in_=xs[:].indirect(picks[0]))
+        gw.append(sb("gw0", [P, BANK], U32))
+        nc.vector.tensor_copy(out=gw[0][:], in_=xw[:].indirect(picks[0]))
+        gs_all = sb("gs", [P, S], U8)
+        nc.vector.tensor_copy(out=gs_all[:], in_=xs[:].indirect(offs_t[:]))
+        gs = [gs_all[:, 0:BANK], gs_all[:, BANK:S]]
 
         w1_bf = sb("w1_bf", [P, H * PACK], BF16)
         w1_view = w1_bf[:].rearrange("p (t m j) -> p m j t", t=4, j=PACK)
@@ -110,29 +110,30 @@ def tile_picked_deeppgappage_none_p_kernel(
                 func=COPY,
             )
         w1_q = quantize("w1", w1_bf[:], H)
-        gs.append(sb("w1_bf", [P, BANK], U8))
-        nc.vector.tensor_copy(out=gs[1][:], in_=xs[:].indirect(picks[1]))
+        gw.append(sb("w1_bf", [P, BANK], U32))
+        nc.vector.tensor_copy(out=gw[1][:], in_=xw[:].indirect(picks[1]))
 
         y = [sb("y%d" % t, [P, S], F32) for t in range(PACK)]
         for t, h in [(0, 0), (1, 0), (0, 1), (1, 1), (2, 0), (2, 1), (3, 0), (3, 1)]:
             b = bank(2 * t + h, [P, BANK])
             mm(b[:], w1_q, slice(P * t, P * (t + 1)), gw[h][:], gs[h][:])
-            if h == 0 and t > 1:
+            if False:
                 nc.vector.tensor_copy(out=y[t][:, BANK * h : BANK * (h + 1)], in_=b[:])
             else:
                 nc.scalar.copy(out=y[t][:, BANK * h : BANK * (h + 1)], in_=b[:])
 
         w2_bf = sb("w2_bf", [P, H * PACK], BF16)
         w2_view = w2_bf[:].rearrange("p (t m j) -> p m j t", t=4, j=PACK)
-        for h in range(2):
-            nc.scalar.copy(
+        for h, copy in enumerate((nc.scalar.copy, nc.vector.tensor_copy)):
+            copy(
                 out=w2_view[:, 64 * h : 64 * h + 64],
                 in_=w2_raw[h][:].rearrange("p j (m t) -> p m j t", t=4),
             )
         w2_q = quantize("w2", w2_bf[:], H)
 
         hb = [bank(t, [P, 2, 256]) for t in range(PACK)]
-        hs = [sb("h%d" % t, [P, V], F32) for t in range(PACK)]
+        h_first = bank(4, [P, 256])
+        hs = {t: sb("h%d" % t, [P, V], F32) for t in range(1, PACK)}
 
         ln = [sb("ln%d" % c, [P, PACK, 512], F32) for c in range(2)]
         u = [sb("u%d" % c, [P, PACK, 256], F32) for c in range(2)]
@@ -140,12 +141,12 @@ def tile_picked_deeppgappage_none_p_kernel(
         for c in range(2):
             for t in range(PACK):
                 win = y[t][:].indirect(n1_t[:, 32 * c : 32 * c + 32])
-                if c == 0 and t < 2:
+                if c == 0 and t < 3:
                     nc.vector.tensor_copy(out=ln[c][:, t, :], in_=win)
                 else:
                     nc.scalar.activation(out=ln[c][:, t, :], in_=win, func=COPY)
-                if True:
-                    ts = slice(t, t + 1)
+                if t % 2 == 1:
+                    ts = slice(t - 1, t + 1)
                     pair = ln[c][:, ts, :].rearrange("p t (v e) -> p (t v) e", e=2)
                     for dst, e in ((u[c], 0), (w[c], 1)):
                         nc.vector.scalar_tensor_tensor(
@@ -158,28 +159,34 @@ def tile_picked_deeppgappage_none_p_kernel(
                         )
             z_bf = sb("z_bf%d" % c, [P, 256 * PACK], BF16)
             nc.vector.tensor_tensor(
-                out=z_bf[:].rearrange("p (c i t) -> p c t i", i=2, t=PACK),
-                in0=u[c][:].rearrange("p t (c i) -> p c t i", i=2),
-                in1=w[c][:].rearrange("p t (c i) -> p c t i", i=2),
+                out=z_bf[:].rearrange("p (c i t) -> p c t i", i=4, t=PACK),
+                in0=u[c][:].rearrange("p t (c i) -> p c t i", i=4),
+                in1=w[c][:].rearrange("p t (c i) -> p c t i", i=4),
                 op=ALU.max,
             )
             z_q = quantize("z%d" % c, z_bf[:], 256)
             for t in range(PACK):
-                mm(hb[t][:, c, :], w2_q, slice(P * t, P * (t + 1)), z_q[0][:], z_q[1][:])
-            nc.scalar.copy(out=hs[0][:, 256 * c : 256 * (c + 1)], in_=hb[0][:, c, :])
+                mm(h_first[:] if (t, c) == (0, 0) else hb[t][:, c, :], w2_q, slice(P * t, P * (t + 1)), z_q[0][:], z_q[1][:])
+        h0 = [sb(name, [P, 256], F32) for name in ("u1", "h0")]
+        for c in range(2):
+            nc.scalar.copy(out=h0[c][:], in_=h_first[:] if c == 0 else hb[0][:, c, :])
         for t in range(1, PACK):
             nc.scalar.copy(out=hs[t][:], in_=hb[t][:].rearrange("p c v -> p (c v)"))
 
         w3_bf = sb("y3", [P, N * PACK], BF16)
         nc.scalar.copy(
-            out=w3_bf[:].rearrange("p (c i j) -> p c j i", i=2, j=PACK),
-            in_=w3_raw[:].rearrange("p j (c i) -> p c j i", i=2),
+            out=w3_bf[:].rearrange("p (c i j) -> p c j i", i=4, j=PACK),
+            in_=w3_raw[:].rearrange("p j (c i) -> p c j i", i=4),
         )
 
         starts = [sum(OUT_CHUNKS[:k]) for k in range(len(OUT_CHUNKS))]
         z2_bf = sb("z2_bf", [P, U, PACK], BF16)
         for t in range(PACK):
-            nc.vector.tensor_copy(out=page[t][:].indirect(n2_t[:]), in_=hs[t][:])
+            if t == 0:
+                for c in range(2):
+                    nc.vector.tensor_copy(out=page[0][:].indirect(n2_t[:, 16 * c : 16 * c + 16]), in_=h0[c][:])
+            else:
+                nc.vector.tensor_copy(out=page[t][:].indirect(n2_t[:]), in_=hs[t][:])
             if t < PACK - 1:
                 nc.scalar.copy(out=z2_bf[:, :, t], in_=page[t][:])
             else:
@@ -190,7 +197,7 @@ def tile_picked_deeppgappage_none_p_kernel(
         w3_q = quantize("w3", w3_bf[:], N, "h3")
         out_view = out.rearrange("(t p) w -> p t w", p=P)
         sums = []
-        nb = 4
+        nb = 5
         for k, wd in enumerate(OUT_CHUNKS):
             cols = slice(starts[k], starts[k] + wd)
             z2_q = quantize("z2_%d" % k, z2_bf[:, cols, :].rearrange("p w t -> p (w t)"), wd)

@@ -102,11 +102,11 @@ def tile_picked_deeppgappage_none_p_kernel(
         gs = [gs_all[:, 0:BANK], gs_all[:, BANK:S]]
 
         w1_bf = sb("w1_bf", [P, H * PACK], BF16)
-        w1_view = w1_bf[:].rearrange("p (t m j) -> p m j t", t=4, j=PACK)
+        w1_view = w1_bf[:].rearrange("p (t m j) -> p m t j", t=4, j=PACK)
         for h in range(2):
             nc.scalar.activation(
                 out=w1_view[:, 64 * h : 64 * h + 64],
-                in_=w1_raw[h][:].rearrange("p j (m t) -> p m j t", t=4),
+                in_=w1_raw[h][:].rearrange("p j (m t) -> p m t j", t=4),
                 func=COPY,
             )
         w1_q = quantize("w1", w1_bf[:], H)
@@ -117,17 +117,17 @@ def tile_picked_deeppgappage_none_p_kernel(
         for t, h in [(0, 0), (1, 0), (0, 1), (1, 1), (2, 0), (2, 1), (3, 0), (3, 1)]:
             b = bank(2 * t + h, [P, BANK])
             mm(b[:], w1_q, slice(P * t, P * (t + 1)), gw[h][:], gs[h][:])
-            if False:
+            if h == 0:
                 nc.vector.tensor_copy(out=y[t][:, BANK * h : BANK * (h + 1)], in_=b[:])
             else:
                 nc.scalar.copy(out=y[t][:, BANK * h : BANK * (h + 1)], in_=b[:])
 
         w2_bf = sb("w2_bf", [P, H * PACK], BF16)
-        w2_view = w2_bf[:].rearrange("p (t m j) -> p m j t", t=4, j=PACK)
-        for h, copy in enumerate((nc.scalar.copy, nc.vector.tensor_copy)):
-            copy(
+        w2_view = w2_bf[:].rearrange("p (t m j) -> p m t j", t=4, j=PACK)
+        for h in range(2):
+            nc.scalar.copy(
                 out=w2_view[:, 64 * h : 64 * h + 64],
-                in_=w2_raw[h][:].rearrange("p j (m t) -> p m j t", t=4),
+                in_=w2_raw[h][:].rearrange("p j (m t) -> p m t j", t=4),
             )
         w2_q = quantize("w2", w2_bf[:], H)
 
@@ -141,12 +141,12 @@ def tile_picked_deeppgappage_none_p_kernel(
         for c in range(2):
             for t in range(PACK):
                 win = y[t][:].indirect(n1_t[:, 32 * c : 32 * c + 32])
-                if c == 0 and t < 3:
+                if c == 0 and t < 2:
                     nc.vector.tensor_copy(out=ln[c][:, t, :], in_=win)
                 else:
                     nc.scalar.activation(out=ln[c][:, t, :], in_=win, func=COPY)
-                if t % 2 == 1:
-                    ts = slice(t - 1, t + 1)
+                if True:
+                    ts = slice(t, t + 1)
                     pair = ln[c][:, ts, :].rearrange("p t (v e) -> p (t v) e", e=2)
                     for dst, e in ((u[c], 0), (w[c], 1)):
                         nc.vector.scalar_tensor_tensor(
@@ -159,9 +159,9 @@ def tile_picked_deeppgappage_none_p_kernel(
                         )
             z_bf = sb("z_bf%d" % c, [P, 256 * PACK], BF16)
             nc.vector.tensor_tensor(
-                out=z_bf[:].rearrange("p (c i t) -> p c t i", i=4, t=PACK),
-                in0=u[c][:].rearrange("p t (c i) -> p c t i", i=4),
-                in1=w[c][:].rearrange("p t (c i) -> p c t i", i=4),
+                out=z_bf[:].rearrange("p (c i t) -> p c t i", i=2, t=PACK),
+                in0=u[c][:].rearrange("p t (c i) -> p c t i", i=2),
+                in1=w[c][:].rearrange("p t (c i) -> p c t i", i=2),
                 op=ALU.max,
             )
             z_q = quantize("z%d" % c, z_bf[:], 256)
@@ -175,8 +175,8 @@ def tile_picked_deeppgappage_none_p_kernel(
 
         w3_bf = sb("y3", [P, N * PACK], BF16)
         nc.scalar.copy(
-            out=w3_bf[:].rearrange("p (c i j) -> p c j i", i=4, j=PACK),
-            in_=w3_raw[:].rearrange("p j (c i) -> p c j i", i=4),
+            out=w3_bf[:].rearrange("p (c i j) -> p c j i", i=2, j=PACK),
+            in_=w3_raw[:].rearrange("p j (c i) -> p c j i", i=2),
         )
 
         starts = [sum(OUT_CHUNKS[:k]) for k in range(len(OUT_CHUNKS))]

@@ -64,9 +64,6 @@ def tile_picked_deeppgappage_none_p_kernel(
                 out=xs[32 * q : 32 * q + 4, :].bitcast(I32),
                 in_=x_scales[0, 4 * q : 4 * q + 4, :].bitcast(I32),
             )
-        nc.sync.dma_start(
-            out=xw[:].bitcast(I32), in_=x_words[0].rearrange("p n t -> p (n t)").bitcast(I32)
-        )
         w1_raw = []
         for h in range(2):
             raw = sb("w1_raw%d" % h, [P, PACK, H // 2], F32)
@@ -74,6 +71,9 @@ def tile_picked_deeppgappage_none_p_kernel(
                 out=raw[:], in_=w1.rearrange("(p j) c -> p j c", j=PACK)[:, :, h * 256 : (h + 1) * 256]
             )
             w1_raw.append(raw)
+        nc.sync.dma_start(
+            out=xw[:].bitcast(I32), in_=x_words[0].rearrange("p n t -> p (n t)").bitcast(I32)
+        )
         nc.sync.dma_start(n1_t[:], n1)
         w2_raw = []
         for h in range(2):
@@ -110,11 +110,11 @@ def tile_picked_deeppgappage_none_p_kernel(
                 func=COPY,
             )
         w1_q = quantize("w1", w1_bf[:], H)
-        gw.append(sb("w1_bf", [P, BANK], U32))
+        gw.append(sb("gw1", [P, BANK], U32))
         nc.vector.tensor_copy(out=gw[1][:], in_=xw[:].indirect(picks[1]))
 
         y = [sb("y%d" % t, [P, S], F32) for t in range(PACK)]
-        for t, h in [(0, 0), (1, 0), (0, 1), (1, 1), (2, 0), (2, 1), (3, 0), (3, 1)]:
+        for t, h in [(t, h) for h in range(2) for t in range(PACK)]:
             b = bank(2 * t + h, [P, BANK])
             mm(b[:], w1_q, slice(P * t, P * (t + 1)), gw[h][:], gs[h][:])
             if h == 0:
@@ -141,7 +141,7 @@ def tile_picked_deeppgappage_none_p_kernel(
         for c in range(2):
             for t in range(PACK):
                 win = y[t][:].indirect(n1_t[:, 32 * c : 32 * c + 32])
-                if c == 0 and t < 2:
+                if c == 0 and t < 3:
                     nc.vector.tensor_copy(out=ln[c][:, t, :], in_=win)
                 else:
                     nc.scalar.activation(out=ln[c][:, t, :], in_=win, func=COPY)

from contextlib import ExitStack

import concourse.mybir as mybir

K, T, S, V, N, H, U = 512, 2048, 1024, 512, 512, 512, 1024
FLOPS = 2 * K * H * S + 2 * H * H * V + 2 * H * N * U

F32 = mybir.dt.float32
BF16 = mybir.dt.bfloat16
I32 = mybir.dt.int32
U32 = mybir.dt.uint32
U16 = mybir.dt.uint16
U8 = mybir.dt.uint8
FP8X4 = mybir.dt.float8_e4m3fn_x4
ALU = mybir.AluOpType
COPY = mybir.ActivationFunctionType.Copy

P = 128
PACK = 4
BANK = 512
OUT_CHUNKS = (128, 256, 256, 256, 128)


def tile_picked_deeppgappage_none_p_kernel(
    tc, x_words, x_scales, w1, w2, mem, w3, res, offs, n1, n2, out
):
    nc = tc.nc
    with ExitStack() as ctx:
        keep = ctx.enter_context(tc.tile_pool(name="keep", bufs=1))
        psum = ctx.enter_context(tc.psum_pool(name="psum", bufs=1))

        def sb(name, shape, dtype):
            return keep.tile(shape, dtype, name=name, align_bytes=64)

        def bank(i, shape):
            return psum.tile(shape, F32, name="bank%d" % (i % 8))

        def quantize(name, grouped, width, codes_name=None):
            codes = sb(codes_name or name + "_codes", [P, width], U32)
            scales = sb(name + "_scales", [P, width], U8)
            nc.vector.quantize_mx(out=codes[:].bitcast(FP8X4), scales=scales[:], in_=grouped)
            return codes, scales

        def mm(dst, w, cols, rhs_codes, rhs_scales):
            nc.tensor.matmul_mx(
                out=dst,
                lhsT=w[0][:, cols].bitcast(FP8X4),
                lhsT_scale=w[1][:, cols],
                rhs=rhs_codes.bitcast(FP8X4),
                rhs_scale=rhs_scales,
                start=True,
                stop=True,
            )

        offs_t = keep.tile([P, S // 16], U16, name="offs_t")
        n1_t = keep.tile([P, S // 16], U16, name="n1_t")
        n2_t = keep.tile([P, V // 16], U16, name="n2_t")
        xw = sb("xw", [P, T], U32)
        xs = sb("xs", [P, T], U8)
        nc.vector.memset(xs[:].bitcast(I32), 0)
        nc.sync.dma_start(offs_t[:], offs)
        for q in range(4):
            nc.sync.dma_start(
                out=xs[32 * q : 32 * q + 4, :].bitcast(I32),
                in_=x_scales[0, 4 * q : 4 * q + 4, :].bitcast(I32),
            )
        w1_raw = []
        for h in range(2):
            raw = sb("w1_raw%d" % h, [P, PACK, H // 2], F32)
            nc.sync.dma_start(
                out=raw[:], in_=w1.rearrange("(p j) c -> p j c", j=PACK)[:, :, h * 256 : (h + 1) * 256]
            )
            w1_raw.append(raw)
        nc.sync.dma_start(
            out=xw[:].bitcast(I32), in_=x_words[0].rearrange("p n t -> p (n t)").bitcast(I32)
        )
        nc.sync.dma_start(n1_t[:], n1)
        w2_raw = []
        for h in range(2):
            raw = sb("w2_raw%d" % h, [P, PACK, H // 2], F32)
            nc.sync.dma_start(
                out=raw[:], in_=w2.rearrange("(p j) c -> p j c", j=PACK)[:, :, h * 256 : (h + 1) * 256]
            )
            w2_raw.append(raw)
        nc.sync.dma_start(n2_t[:], n2)
        w3_raw = sb("w3_raw", [P, PACK, N], F32)
        nc.sync.dma_start(out=w3_raw[:], in_=w3.rearrange("(p j) c -> p j c", j=PACK))
        page = []
        for t in range(PACK):
            pg = sb("page%d" % t, [P, U], F32)
            nc.sync.dma_start(out=pg[:], in_=mem.rearrange("(p t) w -> t p w", t=PACK)[t])
            page.append(pg)
        res_t = sb("res_t", [P, 4, U], F32)
        nc.sync.dma_start(out=res_t[:], in_=res.rearrange("(t p) w -> p t w", p=P))

        gs, gw = [], []
        picks = [offs_t[:, 32 * h : 32 * h + 32] for h in range(2)]
        gw.append(sb("gw0", [P, BANK], U32))
        nc.vector.tensor_copy(out=gw[0][:], in_=xw[:].indirect(picks[0]))
        gs_all = sb("gs", [P, S], U8)
        nc.vector.tensor_copy(out=gs_all[:], in_=xs[:].indirect(offs_t[:]))
        gs = [gs_all[:, 0:BANK], gs_all[:, BANK:S]]

        w1_bf = sb("w1_bf", [P, H * PACK], BF16)
        w1_view = w1_bf[:].rearrange("p (t m j) -> p m t j", t=4, j=PACK)
        for h in range(2):
            nc.scalar.activation(
                out=w1_view[:, 64 * h : 64 * h + 64],
                in_=w1_raw[h][:].rearrange("p j (m t) -> p m t j", t=4),
                func=COPY,
            )
        w1_q = quantize("w1", w1_bf[:], H)
        gw.append(sb("gw1", [P, BANK], U32))
        nc.vector.tensor_copy(out=gw[1][:], in_=xw[:].indirect(picks[1]))

        y = [sb("y%d" % t, [P, S], F32) for t in range(PACK)]
        for t, h in [(t, h) for h in range(2) for t in range(PACK)]:
            b = bank(2 * t + h, [P, BANK])
            mm(b[:], w1_q, slice(P * t, P * (t + 1)), gw[h][:], gs[h][:])
            if h == 0:
                nc.vector.tensor_copy(out=y[t][:, BANK * h : BANK * (h + 1)], in_=b[:])
            else:
                nc.scalar.copy(out=y[t][:, BANK * h : BANK * (h + 1)], in_=b[:])

        w2_bf = sb("w2_bf", [P, H * PACK], BF16)
        w2_view = w2_bf[:].rearrange("p (t m j) -> p m t j", t=4, j=PACK)
        for h in range(2):
            nc.scalar.copy(
                out=w2_view[:, 64 * h : 64 * h + 64],
                in_=w2_raw[h][:].rearrange("p j (m t) -> p m t j", t=4),
            )
        w2_q = quantize("w2", w2_bf[:], H)

        hb = [bank(t, [P, 2, 256]) for t in range(PACK)]
        h_first = bank(4, [P, 256])
        hs = {t: sb("h%d" % t, [P, V], F32) for t in range(1, PACK)}

        ln = [sb("ln%d" % c, [P, PACK, 512], F32) for c in range(2)]
        u = [sb("u%d" % c, [P, PACK, 256], F32) for c in range(2)]
        w = [sb("w%d" % c, [P, PACK, 256], F32) for c in range(2)]
        for c in range(2):
            for t in range(PACK):
                win = y[t][:].indirect(n1_t[:, 32 * c : 32 * c + 32])
                if c == 0 and t < 3:
                    nc.vector.tensor_copy(out=ln[c][:, t, :], in_=win)
                else:
                    nc.scalar.activation(out=ln[c][:, t, :], in_=win, func=COPY)
                if True:
                    ts = slice(t, t + 1)
                    pair = ln[c][:, ts, :].rearrange("p t (v e) -> p (t v) e", e=2)
                    for dst, e in ((u[c], 0), (w[c], 1)):
                        nc.vector.scalar_tensor_tensor(
                            out=dst[:, ts, :].rearrange("p t v -> p (t v)"),
                            in0=pair[:, :, 1 - e],
                            scalar=-0.5,
                            in1=pair[:, :, e],
                            op0=ALU.mult,
                            op1=ALU.add,
                        )
            z_bf = sb("z_bf%d" % c, [P, 256 * PACK], BF16)
            nc.vector.tensor_tensor(
                out=z_bf[:].rearrange("p (c i t) -> p c t i", i=2, t=PACK),
                in0=u[c][:].rearrange("p t (c i) -> p c t i", i=2),
                in1=w[c][:].rearrange("p t (c i) -> p c t i", i=2),
                op=ALU.max,
            )
            z_q = quantize("z%d" % c, z_bf[:], 256)
            for t in range(PACK):
                mm(h_first[:] if (t, c) == (0, 0) else hb[t][:, c, :], w2_q, slice(P * t, P * (t + 1)), z_q[0][:], z_q[1][:])
        h0 = [sb(name, [P, 256], F32) for name in ("u1", "h0")]
        for c in range(2):
            nc.scalar.copy(out=h0[c][:], in_=h_first[:] if c == 0 else hb[0][:, c, :])
        for t in range(1, PACK):
            nc.scalar.copy(out=hs[t][:], in_=hb[t][:].rearrange("p c v -> p (c v)"))

        w3_bf = sb("y3", [P, N * PACK], BF16)
        nc.scalar.copy(
            out=w3_bf[:].rearrange("p (c i j) -> p c j i", i=2, j=PACK),
            in_=w3_raw[:].rearrange("p j (c i) -> p c j i", i=2),
        )

        starts = [sum(OUT_CHUNKS[:k]) for k in range(len(OUT_CHUNKS))]
        z2_bf = sb("z2_bf", [P, U, PACK], BF16)
        for t in range(PACK):
            if t == 0:
                for c in range(2):
                    nc.vector.tensor_copy(out=page[0][:].indirect(n2_t[:, 16 * c : 16 * c + 16]), in_=h0[c][:])
            else:
                nc.vector.tensor_copy(out=page[t][:].indirect(n2_t[:]), in_=hs[t][:])
            if t < PACK - 1:
                nc.scalar.copy(out=z2_bf[:, :, t], in_=page[t][:])
            else:
                for k, wd in enumerate(OUT_CHUNKS):
                    cols = slice(starts[k], starts[k] + wd)
                    nc.scalar.copy(out=z2_bf[:, cols, t], in_=page[t][:, cols])

        w3_q = quantize("w3", w3_bf[:], N, "h3")
        out_view = out.rearrange("(t p) w -> p t w", p=P)
        sums = []
        nb = 5
        for k, wd in enumerate(OUT_CHUNKS):
            cols = slice(starts[k], starts[k] + wd)
            z2_q = quantize("z2_%d" % k, z2_bf[:, cols, :].rearrange("p w t -> p (w t)"), wd)
            per = BANK // wd
            for m0 in range(0, 4, per):
                b = bank(nb, [P, per, wd])
                nb = nb + 1
                for i in range(per):
                    mm(b[:, i, :], w3_q, slice(P * (m0 + i), P * (m0 + i + 1)), z2_q[0][:], z2_q[1][:])
                sums.append((k, m0, per, b))
        o = [sb("o%d" % k, [P, 4, wd], F32) for k, wd in enumerate(OUT_CHUNKS)]
        for k, m0, per, b in sums:
            cols = slice(starts[k], starts[k] + OUT_CHUNKS[k])
            nc.vector.tensor_tensor(
                out=o[k][:, m0 : m0 + per, :], in0=b[:], in1=res_t[:, m0 : m0 + per, cols], op=ALU.add
            )
            nc.sync.dma_start(out=out_view[:, m0 : m0 + per, cols], in_=o[k][:, m0 : m0 + per, :])
